import numpy as np
import ml_dtypes

BF16 = ml_dtypes.bfloat16


def bf(x):
    return np.asarray(x, np.float32).astype(BF16)


def f32(x):
    return np.asarray(x, np.float32)


def f64(x):
    return np.asarray(x).astype(np.float64)


def striped(idx):
    return np.tile(idx.reshape(-1, 16).T, (8, 1))


def rows(idx, k):
    return np.tile(idx, (k, 1))


def look(tab, idx):
    return np.take_along_axis(f64(tab), rows(idx, len(tab)), axis=1)


K, S, D, V, N = 128, 2048, 2, 512, 1024


def setup_inputs():
    return {"tab": f32(np.random.standard_normal((K, S))), "x0": f32(1.0 * np.random.standard_normal((K, V))), "offs": striped(np.random.permutation(S)[:N])}


def reference(tab, x0, offs):
    idx = offs[:16].T.reshape(-1)
    hi = lo = f64(x0)
    for d in range(D):
        hi, lo = np.maximum(hi, look(tab, idx[d * V:(d + 1) * V])), np.minimum(lo, look(tab, idx[d * V:(d + 1) * V]))
    x = hi - lo
    return x

@@ -1,0 +1,33 @@
+import concourse.mybir as mybir
+
+P = 128
+D = 2
+V = 512
+LIST_COLUMNS = V // 16
+
+F32, U16 = mybir.dt.float32, mybir.dt.uint16
+
+
+def tile_lookup_span_out_kernel(tc, tab, x0, offs, out):
+    nc = tc.nc
+    highest, lowest, less = mybir.AluOpType.max, mybir.AluOpType.min, mybir.AluOpType.subtract
+    with tc.tile_pool(name="held", bufs=1) as held:
+        lists = held.tile([P, D * LIST_COLUMNS], U16, name="lists")
+        table = held.tile([P, tab.shape[1]], F32, name="table")
+        own = held.tile([P, V], F32, name="own")
+        nc.sync.dma_start(lists[:], offs)
+        nc.scalar.dma_start(table[:], tab)
+        nc.sync.dma_start(own[:], x0)
+
+        high, low = own, own
+        for d in range(D):
+            entries = lists[:, d * LIST_COLUMNS : (d + 1) * LIST_COLUMNS]
+            higher = held.tile([P, V], F32, name=f"high{d}")
+            lower = held.tile([P, V], F32, name=f"low{d}")
+            nc.vector.tensor_tensor(higher[:], table[:].indirect(entries), high[:], highest)
+            nc.vector.tensor_tensor(lower[:], table[:].indirect(entries), low[:], lowest)
+            high, low = higher, lower
+
+        span = held.tile([P, V], F32, name="span")
+        nc.vector.tensor_tensor(span[:], high[:], low[:], less)
+        nc.sync.dma_start(out, span[:])

@@ -4,6 +4,7 @@ P = 128
 D = 2
 V = 512
 LIST_COLUMNS = V // 16
+HALF = V // 2
 
 F32, U16 = mybir.dt.float32, mybir.dt.uint16
 
@@ -28,6 +29,7 @@ def tile_lookup_span_out_kernel(tc, tab, x0, offs, out):
             nc.vector.tensor_tensor(lower[:], table[:].indirect(entries), low[:], lowest)
             high, low = higher, lower
 
-        span = held.tile([P, V], F32, name="span")
-        nc.vector.tensor_tensor(span[:], high[:], low[:], less)
-        nc.sync.dma_start(out, span[:])
+        for store, c in ((nc.sync, 0), (nc.scalar, HALF)):
+            span = held.tile([P, HALF], F32, name=f"span_{c}")
+            nc.vector.tensor_tensor(span[:], high[:, c : c + HALF], low[:, c : c + HALF], less)
+            store.dma_start(out[:, c : c + HALF], span[:])

@@ -1,10 +1,9 @@
 import concourse.mybir as mybir
 
 P = 128
-D = 2
 V = 512
-LIST_COLUMNS = V // 16
-HALF = V // 2
+LOADS = ((0, V // 2), (V // 2, V))
+STORES = ((0, 3 * V // 4), (3 * V // 4, V))
 
 F32, U16 = mybir.dt.float32, mybir.dt.uint16
 
@@ -13,23 +12,28 @@ def tile_lookup_span_out_kernel(tc, tab, x0, offs, out):
     nc = tc.nc
     highest, lowest, less = mybir.AluOpType.max, mybir.AluOpType.min, mybir.AluOpType.subtract
     with tc.tile_pool(name="held", bufs=1) as held:
-        lists = held.tile([P, D * LIST_COLUMNS], U16, name="lists")
+        lists = held.tile([P, 2 * V // 16], U16, name="lists")
         table = held.tile([P, tab.shape[1]], F32, name="table")
         own = held.tile([P, V], F32, name="own")
         nc.sync.dma_start(lists[:], offs)
+        nc.sync.dma_start(own[:, : V // 2], x0[:, : V // 2])
         nc.scalar.dma_start(table[:], tab)
-        nc.sync.dma_start(own[:], x0)
+        nc.scalar.dma_start(own[:, V // 2 :], x0[:, V // 2 :])
 
-        high, low = own, own
-        for d in range(D):
-            entries = lists[:, d * LIST_COLUMNS : (d + 1) * LIST_COLUMNS]
-            higher = held.tile([P, V], F32, name=f"high{d}")
-            lower = held.tile([P, V], F32, name=f"low{d}")
-            nc.vector.tensor_tensor(higher[:], table[:].indirect(entries), high[:], highest)
-            nc.vector.tensor_tensor(lower[:], table[:].indirect(entries), low[:], lowest)
-            high, low = higher, lower
+        def neighbours(d, begin, end):
+            return table[:].indirect(lists[:, (d * V + begin) // 16 : (d * V + end) // 16])
 
-        for store, c in ((nc.sync, 0), (nc.scalar, HALF)):
-            span = held.tile([P, HALF], F32, name=f"span_{c}")
-            nc.vector.tensor_tensor(span[:], high[:, c : c + HALF], low[:, c : c + HALF], less)
-            store.dma_start(out[:, c : c + HALF], span[:])
+        high = held.tile([P, V], F32, name="high")
+        low = held.tile([P, V], F32, name="low")
+        for begin, end in LOADS:
+            nc.vector.tensor_tensor(high[:, begin:end], neighbours(0, begin, end), own[:, begin:end], highest)
+            nc.vector.tensor_tensor(low[:, begin:end], neighbours(0, begin, end), own[:, begin:end], lowest)
+
+        for begin, end in STORES:
+            top = held.tile([P, end - begin], F32, name=f"top_{begin}")
+            bottom = held.tile([P, end - begin], F32, name=f"bottom_{begin}")
+            span = held.tile([P, end - begin], F32, name=f"span_{begin}")
+            nc.vector.tensor_tensor(top[:], neighbours(1, begin, end), high[:, begin:end], highest)
+            nc.vector.tensor_tensor(bottom[:], neighbours(1, begin, end), low[:, begin:end], lowest)
+            nc.vector.tensor_tensor(span[:], top[:], bottom[:], less)
+            nc.sync.dma_start(out[:, begin:end], span[:])

import concourse.mybir as mybir

P = 128
V = 512
LOADS = ((0, V // 2), (V // 2, V))
STORES = ((0, 3 * V // 4), (3 * V // 4, V))

F32, U16 = mybir.dt.float32, mybir.dt.uint16


def tile_lookup_span_out_kernel(tc, tab, x0, offs, out):
    nc = tc.nc
    highest, lowest, less = mybir.AluOpType.max, mybir.AluOpType.min, mybir.AluOpType.subtract
    with tc.tile_pool(name="held", bufs=1) as held:
        lists = held.tile([P, 2 * V // 16], U16, name="lists")
        table = held.tile([P, tab.shape[1]], F32, name="table")
        own = held.tile([P, V], F32, name="own")
        nc.sync.dma_start(lists[:], offs)
        nc.sync.dma_start(own[:, : V // 2], x0[:, : V // 2])
        nc.scalar.dma_start(table[:], tab)
        nc.scalar.dma_start(own[:, V // 2 :], x0[:, V // 2 :])

        def neighbours(d, begin, end):
            return table[:].indirect(lists[:, (d * V + begin) // 16 : (d * V + end) // 16])

        high = held.tile([P, V], F32, name="high")
        low = held.tile([P, V], F32, name="low")
        for begin, end in LOADS:
            nc.vector.tensor_tensor(high[:, begin:end], neighbours(0, begin, end), own[:, begin:end], highest)
            nc.vector.tensor_tensor(low[:, begin:end], neighbours(0, begin, end), own[:, begin:end], lowest)

        for begin, end in STORES:
            top = held.tile([P, end - begin], F32, name=f"top_{begin}")
            bottom = held.tile([P, end - begin], F32, name=f"bottom_{begin}")
            span = held.tile([P, end - begin], F32, name=f"span_{begin}")
            nc.vector.tensor_tensor(top[:], neighbours(1, begin, end), high[:, begin:end], highest)
            nc.vector.tensor_tensor(bottom[:], neighbours(1, begin, end), low[:, begin:end], lowest)
            nc.vector.tensor_tensor(span[:], top[:], bottom[:], less)
            nc.sync.dma_start(out[:, begin:end], span[:])
